import numpy as np, ml_dtypes
CORES = [2,10,34,50,74,82,98,114,130,138,162,178,202,210,226,242]
N = 16
T = 512
def entries(a): return a.T.reshape(-1)
def pack(v, P): return np.ascontiguousarray(np.asarray(v, np.int32).reshape(-1, P).T)
def lists(rng, how):
    n = rng.integers(0, T + 1, N)
    if how == "none": n[rng.integers(N)] = 0; n[0] = 0
    if how == "full": n[:] = T
    if how == "one": n[:] = 1
    if how == "lone": z = int(rng.integers(N)); n[:] = 0; n[z] = int(rng.integers(1, T + 1))
    if how == "void": n[:] = 0
    return {"ln": np.broadcast_to(pack(np.concatenate([n, np.zeros(32 - N, np.int64)]), 16), (N, 16, 2)).copy()}
def setup_inputs(rng):
    return dict({"x": rng.standard_normal((N, 128, T), dtype=np.float32).astype(ml_dtypes.bfloat16)}, **lists(rng, "uniform"))
def setup_inputs_full(rng):
    d = setup_inputs(rng); d.update(lists(rng, "full"))
    for k in ("x",): d[k] = (d[k].astype(np.float32) * 1048576.0).astype(d[k].dtype)
    return d
def setup_inputs_lone(rng):
    d = setup_inputs(rng); d.update(lists(rng, "lone"))
    for k in ("x",): d[k] = (d[k].astype(np.float32) * (1 / 1024.0)).astype(d[k].dtype)
    return d
def setup_inputs_none(rng):
    d = setup_inputs(rng); d.update(lists(rng, "none"))
    return d
def setup_inputs_one(rng):
    d = setup_inputs(rng); d.update(lists(rng, "one"))
    return d
def setup_inputs_void(rng):
    d = setup_inputs(rng); d.update(lists(rng, "void"))
    return d
def check_inputs(x):
    bad = []
    if x["ln"].min() < 0 or x["ln"].max() >= T + 1: bad.append("ln out of range")
    if entries(x["ln"][0])[N:].any(): bad.append("an entry from N on isn't 0")
    if not all(np.array_equal(a, x["ln"][0]) for a in x["ln"]): bad.append("ln isn't alike on all ranks")
    return bad
def reference(x, ln):
    n = entries(ln[0]); got = np.concatenate([x[r][:, :n[r]] for r in range(N)], axis=1)
    y = np.zeros((128, N * T), x.dtype); y[:, :got.shape[1]] = got
    return {"y": np.broadcast_to(y, (N, 128, N * T))}

@@ -1,0 +1,237 @@
+from concourse.bass import DstId, RemoteDMATransfer
+from concourse.mybir import AluOpType, ActivationFunctionType
+
+N = 16
+W = 512
+Z = 8
+QC = W // 16
+
+SCRATCH = {
+    "win": ("sbuf", [128, Z + N * W], "bfloat16"),
+    "outb": ("sbuf", [128, N * W], "bfloat16"),
+    "offs": ("sbuf", [128, N * QC], "uint16"),
+    "lnsb": ("sbuf", [48, 2], "int32"),
+    "nf": ("sbuf", [48, 1], "float32"),
+    "tri": ("sbuf", [16, 48], "float32"),
+    "kcol": ("sbuf", [48, 1], "float32"),
+    "scol": ("sbuf", [48, 1], "float32"),
+    "ei": ("sbuf", [48, 1], "int32"),
+    "abi": ("sbuf", [48, 2], "int32"),
+    "abf": ("sbuf", [48, 2], "float32"),
+    "ones": ("sbuf", [48, W], "float32"),
+    "rhs": ("sbuf", [48, W], "float32"),
+    "lhs": ("sbuf", [48, 128], "float32"),
+    "pcol": ("sbuf", [128, 1], "int32"),
+    "pmi": ("sbuf", [128, 1], "int32"),
+    "mcol": ("sbuf", [128, 1], "float32"),
+    "psa": ("psum", [128, 512], "float32"),
+    "psb": ("psum", [128, 512], "float32"),
+}
+SEMAPHORES = ["sx", "sln", "st", "vs", "gs", "pe", "sent"] + ["arr%d" % s for s in range(N)] + \
+             ["done%d" % i for i in range(N // 2)]
+
+_PLAN = {}
+
+
+def _plan(cores, topo):
+    if "p" in _PLAN:
+        return _PLAN["p"]
+    n = len(cores)
+    world = range(topo.CORES_PER_HOST * (1 + max(topo.host(c) for c in cores)))
+
+    def ck(c):
+        return (topo.host(c), topo.chip(c))
+
+    chipc = {}
+    for c in world:
+        chipc.setdefault(ck(c), []).append(c)
+    mate = {}
+    for a in chipc:
+        for b in chipc:
+            if topo.mates(chipc[a][0], chipc[b][0]):
+                mate[a] = b
+    busy = set(ck(c) for c in cores)
+    load = {}
+
+    def route(a, b):
+        d = topo.die(a)
+        if ck(a) == ck(b):
+            return []
+        if topo.same_plane(a, b):
+            return [("out", ck(a), d), ("in", ck(b), d)]
+        r = [("mate", ck(a), d)]
+        if mate[ck(a)] != ck(b):
+            r += [("out", mate[ck(a)], d), ("in", ck(b), d)]
+        return r
+
+    def charge(a, b):
+        for l in route(a, b):
+            load[l] = load.get(l, 0) + 1
+
+    pools = {}
+    taken = set()
+    for s, cs in enumerate(cores):
+        own = chipc[ck(cs)]
+        cross = [d for d in range(n) if d != s and not topo.same_plane(cs, cores[d])]
+        far = [d for d in cross if not topo.mates(cs, cores[d])]
+        relay = []
+        if mate[ck(cs)] in busy and 2 * len(cross) > n - 1:
+            for k in sorted(chipc):
+                if (k[0] == topo.host(cs) and k not in busy and mate[k] not in busy and k not in taken
+                        and all(topo.same_plane(chipc[k][0], cores[d]) for d in far)):
+                    taken.add(k)
+                    for die in sorted(set(topo.die(c) for c in chipc[k])):
+                        relay += [c for c in chipc[k] if topo.die(c) == die][:2]
+                    break
+        for c in relay:
+            charge(cs, c)
+        pools[s] = (own, relay, set(far) if relay else set())
+    work = {c: 1 for c in cores}
+    send = {}
+    origin = {}
+    pairs = [(s, (s + dl) % n) for dl in range(1, n) for s in range(n)]
+    pairs.sort(key=lambda p: topo.same_plane(cores[p[0]], cores[p[1]]))
+    for s, d in pairs:
+        own, relay, far = pools[s]
+        cand = relay if d in far else [c for c in own if topo.may_write(c, cores[d])]
+        if topo.mates(cores[s], cores[d]):
+            cand = [cores[s]]
+        best = min(cand, key=lambda c: (max(load.get(l, 0) for l in route(c, cores[d])), work.get(c, 0), c))
+        charge(best, cores[d])
+        work[best] = work.get(best, 0) + 1
+        send.setdefault(best, (s, []))[1].append(d)
+        origin[(s, d)] = best
+    helpers = {}
+    for s, cs in enumerate(cores):
+        hs = sorted((c for c in send if send[c][0] == s and c != cs), key=lambda c: (-len(send[c][1]), c))
+        helpers[s] = ([c for c in hs if ck(c) != ck(cs)], [c for c in hs if ck(c) == ck(cs)])
+    _PLAN["p"] = (send, helpers, origin)
+    return _PLAN["p"]
+
+
+def _bits(m):
+    return bin(m).count("1")
+
+
+def _slot(T, s):
+    a = Z + W * (N - 1 - s)
+    return T.win[:, a:a + W]
+
+
+def _fan(g, core, T, topo, s, targets):
+    if not targets:
+        return 0
+    m = topo.mask(core, targets[0])
+    ids = []
+    for t in targets:
+        rid, pid = topo.addr(t, core)
+        ids.append(DstId(rid=rid, pnc=pid))
+    tr = RemoteDMATransfer(dst_ids=ids, dma_engine_mask=m, remote_sem=T.sem["arr%d" % s],
+                           srcs=[_slot(T, s)], dsts=[_slot(T, s) for t in targets], alu_op=0)
+    g.remote_dma_fused([tr], local_sem=T.sem.sent)
+    return _bits(m)
+
+
+def rank_program(g, core, T, topo):
+    cores = list(T.cores)
+    send, helpers, origin = _plan(cores, topo)
+    rank = T.rank_of(core)
+    if rank is None:
+        if core not in send:
+            return
+        s, dests = send[core]
+        g.wait_ge(T.sem["arr%d" % s], _bits(topo.mask(cores[s], core)))
+        left = _fan(g, core, T, topo, s, [cores[d] for d in dests])
+        g.wait_ge(T.sem.sent, left)
+        return
+
+    A = AluOpType
+    v, sc, pe, sy = g.vector, g.scalar, g.tensor, g.sync
+    sem = T.sem
+
+    sy.dma_start(_slot(T, rank), T.x[:, :]).then_inc(sem.sx, 16)
+    for t in range(3):
+        sc.dma_start(T.lnsb[16 * t:16 * t + 16, :], T.ln[:, :]).then_inc(sem.sln, 16)
+
+    vc = [0]
+
+    def V(ins):
+        ins.then_inc(sem.vs, 1)
+        vc[0] += 1
+        v.wait_ge(sem.vs, vc[0])
+
+    gc = [0]
+
+    def G(ins):
+        ins.then_inc(sem.gs, 1)
+        gc[0] += 1
+        g.wait_ge(sem.gs, gc[0])
+
+    V(v.memset(T.tri[:, :], 1.0))
+    V(v.memset(T.kcol[:, :], float(W)))
+    G(g.iota(T.pcol[:, 0:1], [[0, 1]], 0, 1))
+    G(g.iota(T.lhs[32:48, :], [[0, 8], [1, 16]], 0, 0, allow_small_or_imprecise_dtypes=True))
+    g.wait_ge(sem.vs, 2)
+    G(g.affine_select(T.tri[:, :], T.tri[:, :], [[0, 3], [1, 16]], A.is_ge, 0.0, 0, -1))
+    g_tri = gc[0]
+    G(g.affine_select(T.kcol[:, :], T.kcol[:, :], [[0, 1]], A.not_equal, 16896.0, -(N - 1), 1))
+    G(g.affine_select(T.kcol[:, :], T.kcol[:, :], [[0, 1]], A.not_equal, 16896.0, -(32 + N - 1), 1))
+
+    g.wait_ge(sem.sx, 16)
+    far_h, near_h = helpers[rank]
+    left = _fan(g, core, T, topo, rank, far_h)
+    left += _fan(g, core, T, topo, rank, near_h)
+    if core in send:
+        left += _fan(g, core, T, topo, rank, [cores[d] for d in send[core][1]])
+
+    V(v.memset(T.lhs[0:32, :], 1.0))
+    V(v.memset(T.win[:, 0:Z], 0.0))
+    V(v.memset(T.ones[:, :], 1.0))
+    V(v.tensor_tensor_scan(T.rhs[:, :], T.ones[:, :], T.ones[:, :], -1.0, A.mult, A.add))
+    v.wait_ge(sem.gs, 1)
+    V(v.tensor_scalar(T.pmi[:, :], T.pcol[:, :], 15, None, A.bitwise_and))
+    V(v.tensor_scalar(T.mcol[:, :], T.pmi[:, :], float(Z + W * (N - 1)), None, A.add))
+    v.wait_ge(sem.sln, 48)
+    V(v.tensor_copy(T.nf[:, :], T.lnsb[:, 0:1]))
+    pe.wait_ge(sem.vs, vc[0])
+    pe.wait_ge(sem.gs, g_tri)
+    pe.matmul(T.psa[0:48, 0:1], T.tri[0:16, 0:48], T.nf[0:16, 0:1], True, True).then_inc(sem.pe, 1)
+    v.wait_ge(sem.gs, gc[0])
+    V(v.tensor_scalar(T.scol[:, :], T.nf[:, :], T.kcol[:, 0:1], -1.0, A.add, A.mult))
+    v.wait_ge(sem.pe, 1)
+    V(v.tensor_copy(T.ei[:, :], T.psa[0:48, 0:1]))
+    V(v.tensor_scalar(T.abi[:, 0:1], T.ei[:, :], 4, None, A.arith_shift_right))
+    V(v.tensor_scalar(T.abi[:, 1:2], T.ei[:, :], 15, None, A.bitwise_and))
+    V(v.tensor_copy(T.abf[:, :], T.abi[:, :]))
+    V(v.tensor_scalar(T.rhs[0:16, :], T.rhs[0:16, :], T.abf[0:16, 0:1], T.scol[0:16, 0:1], A.is_gt, A.mult))
+    V(v.tensor_scalar(T.rhs[32:48, :], T.rhs[32:48, :], T.abf[32:48, 0:1], T.scol[32:48, 0:1], A.is_equal, A.mult))
+    V(v.tensor_scalar(T.lhs[32:48, :], T.lhs[32:48, :], T.abf[32:48, 1:2], None, A.is_ge))
+    pe.wait_ge(sem.vs, vc[0])
+    pe.matmul(T.psb[:, :], T.lhs[0:48, :], T.rhs[0:48, :], True, True).then_inc(sem.pe, 1)
+    v.wait_ge(sem.pe, 2)
+    V(v.tensor_scalar(T.offs[:, :], T.psb[:, :], T.mcol[:, 0:1], 0.0, A.add, A.max))
+
+    sc.wait_ge(sem.vs, vc[0])
+    seen = {0: set(), 1: set()}
+    for k in range(N - 1, -1, -1):
+        e = k % 2
+        q = v if e else sc
+        for s in range(k, N):
+            if s not in seen[e]:
+                seen[e].add(s)
+                if s == rank:
+                    q.wait_ge(sem.sx, 16)
+                else:
+                    q.wait_ge(sem["arr%d" % s], _bits(topo.mask(origin[(s, rank)], core)))
+        src = T.win[:, 0:Z + W * (N - k)].indirect(T.offs[:, QC * k:QC * (k + 1)])
+        dst = T.outb[:, W * k:W * (k + 1)]
+        if e:
+            v.tensor_copy(dst, src).then_inc(sem["done%d" % (k // 2)], 1)
+        else:
+            sc.activation(dst, src, ActivationFunctionType.Copy).then_inc(sem["done%d" % (k // 2)], 1)
+
+    for i in range(N // 2 - 1, -1, -1):
+        sy.wait_ge(sem["done%d" % i], 2)
+        sy.dma_start(T.y[:, 2 * W * i:2 * W * (i + 1)], T.outb[:, 2 * W * i:2 * W * (i + 1)]).then_inc(sem.st, 16)
+    sy.wait_ge(sem.st, 16 * (N // 2))
+    g.wait_ge(sem.sent, left)

@@ -5,9 +5,12 @@ N = 16
 W = 512
 Z = 8
 QC = W // 16
+LOW = 5
+PAIR = 6
 
 SCRATCH = {
     "win": ("sbuf", [128, Z + N * W], "bfloat16"),
+    "xd": ("dram", [128, W], "bfloat16"),
     "outb": ("sbuf", [128, N * W], "bfloat16"),
     "offs": ("sbuf", [128, N * QC], "uint16"),
     "lnsb": ("sbuf", [48, 2], "int32"),
@@ -27,7 +30,7 @@ SCRATCH = {
     "psa": ("psum", [128, 512], "float32"),
     "psb": ("psum", [128, 512], "float32"),
 }
-SEMAPHORES = ["sx", "sln", "st", "vs", "gs", "pe", "sent"] + ["arr%d" % s for s in range(N)] + \
+SEMAPHORES = ["sx", "sxd", "sln", "st", "vs", "gs", "pe", "sent"] + ["arr%d" % s for s in range(N)] + \
              ["done%d" % i for i in range(N // 2)]
 
 _PLAN = {}
@@ -50,7 +53,9 @@ def _plan(cores, topo):
         for b in chipc:
             if topo.mates(chipc[a][0], chipc[b][0]):
                 mate[a] = b
-    busy = set(ck(c) for c in cores)
+    busy = {}
+    for r, c in enumerate(cores):
+        busy[ck(c)] = r
     load = {}
 
     def route(a, b):
@@ -68,44 +73,77 @@ def _plan(cores, topo):
         for l in route(a, b):
             load[l] = load.get(l, 0) + 1
 
+    fwd = {}
+    jobs = []
+    origin = {}
+    skip = set()
+    low = [s for s in range(n) if mate[ck(cores[s])] not in busy][:LOW]
+    for d, cd in enumerate(cores):
+        m = mate[ck(cd)]
+        if m in busy:
+            e = busy[m]
+            if d < e:
+                ls = [s for s in range(n) if s not in (d, e)][:PAIR]
+                for i, s in enumerate(ls):
+                    a, b = (e, d) if i % 3 == 1 else (d, e)
+                    fwd.setdefault(cores[a], []).append((s, b))
+                    origin[(s, cores[b])] = cores[a]
+                    skip.add((s, b))
+                    charge(cores[a], cores[b])
+        else:
+            door = [c for c in chipc[m] if topo.may_write(c, cd)]
+            for s in low:
+                if s == d:
+                    continue
+                f = min(door, key=lambda c: (len(fwd.get(c, [])), load.get(("mate", m, topo.die(c)), 0), c))
+                fwd.setdefault(f, []).append((s, d))
+                origin[(s, cd)] = f
+                skip.add((s, d))
+                charge(f, cd)
+                jobs.append((s, f))
+    for dl in range(1, n):
+        for s in range(n):
+            d = (s + dl) % n
+            if (s, d) not in skip:
+                jobs.append((s, cores[d]))
+
     pools = {}
     taken = set()
     for s, cs in enumerate(cores):
-        own = chipc[ck(cs)]
-        cross = [d for d in range(n) if d != s and not topo.same_plane(cs, cores[d])]
-        far = [d for d in cross if not topo.mates(cs, cores[d])]
+        tg = [t for (a, t) in jobs if a == s]
+        far = [t for t in tg if not topo.same_plane(cs, t) and not topo.mates(cs, t)]
         relay = []
-        if mate[ck(cs)] in busy and 2 * len(cross) > n - 1:
+        if mate[ck(cs)] in busy and 2 * len(far) > len(tg):
             for k in sorted(chipc):
                 if (k[0] == topo.host(cs) and k not in busy and mate[k] not in busy and k not in taken
-                        and all(topo.same_plane(chipc[k][0], cores[d]) for d in far)):
+                        and all(topo.same_plane(chipc[k][0], t) for t in far)):
                     taken.add(k)
                     for die in sorted(set(topo.die(c) for c in chipc[k])):
                         relay += [c for c in chipc[k] if topo.die(c) == die][:2]
                     break
         for c in relay:
             charge(cs, c)
-        pools[s] = (own, relay, set(far) if relay else set())
+        pools[s] = (chipc[ck(cs)], relay, set(far) if relay else set())
     work = {c: 1 for c in cores}
     send = {}
-    origin = {}
-    pairs = [(s, (s + dl) % n) for dl in range(1, n) for s in range(n)]
-    pairs.sort(key=lambda p: topo.same_plane(cores[p[0]], cores[p[1]]))
-    for s, d in pairs:
+    jobs.sort(key=lambda p: topo.same_plane(cores[p[0]], p[1]))
+    for s, t in jobs:
         own, relay, far = pools[s]
-        cand = relay if d in far else [c for c in own if topo.may_write(c, cores[d])]
-        if topo.mates(cores[s], cores[d]):
+        cand = relay if t in far else [c for c in own if topo.may_write(c, t)]
+        if topo.mates(cores[s], t):
             cand = [cores[s]]
-        best = min(cand, key=lambda c: (max(load.get(l, 0) for l in route(c, cores[d])), work.get(c, 0), c))
-        charge(best, cores[d])
+        best = min(cand, key=lambda c: (max(load.get(l, 0) for l in route(c, t)), work.get(c, 0), c))
+        charge(best, t)
         work[best] = work.get(best, 0) + 1
-        send.setdefault(best, (s, []))[1].append(d)
-        origin[(s, d)] = best
+        send.setdefault(best, (s, []))[1].append(t)
+        origin[(s, t)] = best
     helpers = {}
     for s, cs in enumerate(cores):
         hs = sorted((c for c in send if send[c][0] == s and c != cs), key=lambda c: (-len(send[c][1]), c))
         helpers[s] = ([c for c in hs if ck(c) != ck(cs)], [c for c in hs if ck(c) == ck(cs)])
-    _PLAN["p"] = (send, helpers, origin)
+    for f in fwd:
+        fwd[f].sort(key=lambda p: -p[0])
+    _PLAN["p"] = (send, helpers, fwd, origin)
     return _PLAN["p"]
 
 
@@ -118,7 +156,7 @@ def _slot(T, s):
     return T.win[:, a:a + W]
 
 
-def _fan(g, core, T, topo, s, targets):
+def _fan(g, core, T, topo, s, targets, to_helpers):
     if not targets:
         return 0
     m = topo.mask(core, targets[0])
@@ -127,28 +165,42 @@ def _fan(g, core, T, topo, s, targets):
         rid, pid = topo.addr(t, core)
         ids.append(DstId(rid=rid, pnc=pid))
     tr = RemoteDMATransfer(dst_ids=ids, dma_engine_mask=m, remote_sem=T.sem["arr%d" % s],
-                           srcs=[_slot(T, s)], dsts=[_slot(T, s) for t in targets], alu_op=0)
+                           srcs=[T.xd[:, :]], dsts=[T.xd[:, :] if to_helpers else _slot(T, s) for t in targets], alu_op=0)
     g.remote_dma_fused([tr], local_sem=T.sem.sent)
     return _bits(m)
 
 
+def _pass_on(g, core, T, topo, cores, todo, origin):
+    left = 0
+    for s, d in todo:
+        g.wait_ge(T.sem["arr%d" % s], _bits(topo.mask(origin[(s, core)], core)))
+        rid, pid = topo.addr(cores[d], core)
+        m = topo.mask(core, cores[d])
+        g.remote_dma(_slot(T, s), _slot(T, s), T.sem["arr%d" % s], T.sem.sent, pid, rid, m)
+        left += _bits(m)
+    return left
+
+
 def rank_program(g, core, T, topo):
     cores = list(T.cores)
-    send, helpers, origin = _plan(cores, topo)
+    send, helpers, fwd, origin = _plan(cores, topo)
     rank = T.rank_of(core)
     if rank is None:
-        if core not in send:
-            return
-        s, dests = send[core]
-        g.wait_ge(T.sem["arr%d" % s], _bits(topo.mask(cores[s], core)))
-        left = _fan(g, core, T, topo, s, [cores[d] for d in dests])
-        g.wait_ge(T.sem.sent, left)
+        if core in send:
+            s, targets = send[core]
+            g.wait_ge(T.sem["arr%d" % s], _bits(topo.mask(cores[s], core)))
+            left = _fan(g, core, T, topo, s, targets, False)
+            g.wait_ge(T.sem.sent, left)
+        elif core in fwd:
+            left = _pass_on(g, core, T, topo, cores, fwd[core], origin)
+            g.wait_ge(T.sem.sent, left)
         return
 
     A = AluOpType
     v, sc, pe, sy = g.vector, g.scalar, g.tensor, g.sync
     sem = T.sem
 
+    sy.dma_start(T.xd[:, :], T.x[:, :]).then_inc(sem.sxd, 16)
     sy.dma_start(_slot(T, rank), T.x[:, :]).then_inc(sem.sx, 16)
     for t in range(3):
         sc.dma_start(T.lnsb[16 * t:16 * t + 16, :], T.ln[:, :]).then_inc(sem.sln, 16)
@@ -177,12 +229,13 @@ def rank_program(g, core, T, topo):
     G(g.affine_select(T.kcol[:, :], T.kcol[:, :], [[0, 1]], A.not_equal, 16896.0, -(N - 1), 1))
     G(g.affine_select(T.kcol[:, :], T.kcol[:, :], [[0, 1]], A.not_equal, 16896.0, -(32 + N - 1), 1))
 
-    g.wait_ge(sem.sx, 16)
+    g.wait_ge(sem.sxd, 16)
     far_h, near_h = helpers[rank]
-    left = _fan(g, core, T, topo, rank, far_h)
-    left += _fan(g, core, T, topo, rank, near_h)
+    left = _fan(g, core, T, topo, rank, far_h, True)
+    left += _fan(g, core, T, topo, rank, near_h, True)
     if core in send:
-        left += _fan(g, core, T, topo, rank, [cores[d] for d in send[core][1]])
+        left += _fan(g, core, T, topo, rank, send[core][1], False)
+    left += _pass_on(g, core, T, topo, cores, fwd.get(core, []), origin)
 
     V(v.memset(T.lhs[0:32, :], 1.0))
     V(v.memset(T.win[:, 0:Z], 0.0))
@@ -222,7 +275,7 @@ def rank_program(g, core, T, topo):
                 if s == rank:
                     q.wait_ge(sem.sx, 16)
                 else:
-                    q.wait_ge(sem["arr%d" % s], _bits(topo.mask(origin[(s, rank)], core)))
+                    q.wait_ge(sem["arr%d" % s], _bits(topo.mask(origin[(s, core)], core)))
         src = T.win[:, 0:Z + W * (N - k)].indirect(T.offs[:, QC * k:QC * (k + 1)])
         dst = T.outb[:, W * k:W * (k + 1)]
         if e:

@@ -7,10 +7,12 @@ Z = 8
 QC = W // 16
 LOW = 5
 PAIR = 6
+H = 2
+WH = W // H
 
 SCRATCH = {
     "win": ("sbuf", [128, Z + N * W], "bfloat16"),
-    "xd": ("dram", [128, W], "bfloat16"),
+    "xd": ("dram", [H, 128, WH], "bfloat16"),
     "outb": ("sbuf", [128, N * W], "bfloat16"),
     "offs": ("sbuf", [128, N * QC], "uint16"),
     "lnsb": ("sbuf", [48, 2], "int32"),
@@ -30,10 +32,14 @@ SCRATCH = {
     "psa": ("psum", [128, 512], "float32"),
     "psb": ("psum", [128, 512], "float32"),
 }
-SEMAPHORES = ["sx", "sxd", "sln", "st", "vs", "gs", "pe", "sent"] + ["arr%d" % s for s in range(N)] + \
-             ["done%d" % i for i in range(N // 2)]
+SEMAPHORES = ["sx", "sxd", "sln", "st", "vs", "gs", "pe", "sent", "last0", "last1"] + \
+             ["arr%d" % s for s in range(N)] + ["done%d" % i for i in range(1, N // 2)]
 
 _PLAN = {}
+
+
+def _bits(m):
+    return bin(m).count("1")
 
 
 def _plan(cores, topo):
@@ -69,38 +75,43 @@ def _plan(cores, topo):
             r += [("out", mate[ck(a)], d), ("in", ck(b), d)]
         return r
 
-    def charge(a, b):
+    def charge(a, b, u):
         for l in route(a, b):
-            load[l] = load.get(l, 0) + 1
+            load[l] = load.get(l, 0) + u
 
     fwd = {}
     jobs = []
-    origin = {}
     skip = set()
-    low = [s for s in range(n) if mate[ck(cores[s])] not in busy][:LOW]
+    low = list(range(n))[:LOW]
+    pairs = []
     for d, cd in enumerate(cores):
         m = mate[ck(cd)]
         if m in busy:
-            e = busy[m]
-            if d < e:
-                ls = [s for s in range(n) if s not in (d, e)][:PAIR]
-                for i, s in enumerate(ls):
-                    a, b = (e, d) if i % 3 == 1 else (d, e)
-                    fwd.setdefault(cores[a], []).append((s, b))
-                    origin[(s, cores[b])] = cores[a]
-                    skip.add((s, b))
-                    charge(cores[a], cores[b])
-        else:
-            door = [c for c in chipc[m] if topo.may_write(c, cd)]
-            for s in low:
-                if s == d:
-                    continue
-                f = min(door, key=lambda c: (len(fwd.get(c, [])), load.get(("mate", m, topo.die(c)), 0), c))
-                fwd.setdefault(f, []).append((s, d))
-                origin[(s, cd)] = f
-                skip.add((s, d))
-                charge(f, cd)
-                jobs.append((s, f))
+            if d < busy[m]:
+                pairs.append((d, busy[m]))
+            continue
+        door = [c for c in chipc[m] if topo.may_write(c, cd)]
+        for s in low:
+            if s == d:
+                continue
+            f = min(door, key=lambda c: (len(fwd.get(c, [])), load.get(("mate", m, topo.die(c)), 0), c))
+            fwd.setdefault(f, []).append((s, d))
+            skip.add((s, d))
+            charge(f, cd, H)
+            jobs.append((s, f))
+
+    def cross(r):
+        tg = [t for (a, t) in jobs if a == r] + [cores[q] for q in range(n) if q != r and (r, q) not in skip]
+        return sum(1 for t in tg if not topo.same_plane(cores[r], t) and not topo.mates(cores[r], t))
+
+    for d, e in pairs:
+        f, o = (d, e) if cross(d) > cross(e) else (e, d)
+        ls = [s for s in range(n) if s not in (d, e)][:PAIR]
+        for i, s in enumerate(ls):
+            a, b = (f, o) if i % 3 == 1 else (o, f)
+            fwd.setdefault(cores[a], []).append((s, b))
+            skip.add((s, b))
+            charge(cores[a], cores[b], H)
     for dl in range(1, n):
         for s in range(n):
             d = (s + dl) % n
@@ -109,6 +120,7 @@ def _plan(cores, topo):
 
     pools = {}
     taken = set()
+    half = {}
     for s, cs in enumerate(cores):
         tg = [t for (a, t) in jobs if a == s]
         far = [t for t in tg if not topo.same_plane(cs, t) and not topo.mates(cs, t)]
@@ -121,34 +133,55 @@ def _plan(cores, topo):
                     for die in sorted(set(topo.die(c) for c in chipc[k])):
                         relay += [c for c in chipc[k] if topo.die(c) == die][:2]
                     break
-        for c in relay:
-            charge(cs, c)
-        pools[s] = (chipc[ck(cs)], relay, set(far) if relay else set())
-    work = {c: 1 for c in cores}
+        for i, c in enumerate(relay):
+            charge(cs, c, 1)
+            half[c] = i % H
+        probe = chipc[mate[ck(cs)]][0]
+        own = sorted(chipc[ck(cs)], key=lambda c: (not topo.may_write(c, probe), topo.die(c), c))
+        for i, c in enumerate(own):
+            half[c] = i % H
+        pools[s] = (own, relay, set(far) if relay else set())
+    work = {c: H for c in cores}
     send = {}
     jobs.sort(key=lambda p: topo.same_plane(cores[p[0]], p[1]))
     for s, t in jobs:
         own, relay, far = pools[s]
-        cand = relay if t in far else [c for c in own if topo.may_write(c, t)]
-        if topo.mates(cores[s], t):
-            cand = [cores[s]]
-        best = min(cand, key=lambda c: (max(load.get(l, 0) for l in route(c, t)), work.get(c, 0), c))
-        charge(best, t)
-        work[best] = work.get(best, 0) + 1
-        send.setdefault(best, (s, []))[1].append(t)
-        origin[(s, t)] = best
+        for h in range(H):
+            if topo.mates(cores[s], t):
+                cand = [cores[s]]
+            elif t in far:
+                cand = [c for c in relay if half[c] == h]
+            else:
+                cand = [c for c in own if topo.may_write(c, t) and (c == cores[s] or half[c] == h)]
+            best = min(cand, key=lambda c: (max(load.get(l, 0) for l in route(c, t)), work.get(c, 0), c))
+            charge(best, t, 1)
+            work[best] = work.get(best, 0) + 1
+            send.setdefault(best, (s, {}))[1].setdefault(h, []).append(t)
     helpers = {}
     for s, cs in enumerate(cores):
-        hs = sorted((c for c in send if send[c][0] == s and c != cs), key=lambda c: (-len(send[c][1]), c))
-        helpers[s] = ([c for c in hs if ck(c) != ck(cs)], [c for c in hs if ck(c) == ck(cs)])
+        grp = ({}, {})
+        for c in sorted(send):
+            if send[c][0] == s and c != cs:
+                grp[ck(c) == ck(cs)].setdefault(half[c], []).append(c)
+        helpers[s] = grp
     for f in fwd:
         fwd[f].sort(key=lambda p: -p[0])
-    _PLAN["p"] = (send, helpers, fwd, origin)
+    need = {}
+    for c in send:
+        s, hh = send[c]
+        for h in hh:
+            for t in hh[h]:
+                need[(s, t)] = need.get((s, t), 0) + _bits(topo.mask(c, t)) // len(hh)
+    for s, cs in enumerate(cores):
+        for grp in helpers[s]:
+            for h in grp:
+                for c in grp[h]:
+                    need[(s, c)] = _bits(topo.mask(cs, c)) // len(grp)
+    for f in fwd:
+        for s, d in fwd[f]:
+            need[(s, cores[d])] = need.get((s, cores[d]), 0) + _bits(topo.mask(f, cores[d]))
+    _PLAN["p"] = (send, helpers, fwd, need)
     return _PLAN["p"]
-
-
-def _bits(m):
-    return bin(m).count("1")
 
 
 def _slot(T, s):
@@ -156,24 +189,38 @@ def _slot(T, s):
     return T.win[:, a:a + W]
 
 
-def _fan(g, core, T, topo, s, targets, to_helpers):
-    if not targets:
+def _part(T, s, h):
+    a = Z + W * (N - 1 - s) + WH * h
+    return T.win[:, a:a + WH]
+
+
+def _split(m, parts):
+    bl = [1 << i for i in range(m.bit_length()) if (m >> i) & 1]
+    k = len(bl) // parts
+    return [sum(bl[i * k:(i + 1) * k]) for i in range(parts)]
+
+
+def _fan(g, core, T, topo, s, hh, to_helpers):
+    if not hh:
         return 0
-    m = topo.mask(core, targets[0])
-    ids = []
-    for t in targets:
-        rid, pid = topo.addr(t, core)
-        ids.append(DstId(rid=rid, pnc=pid))
-    tr = RemoteDMATransfer(dst_ids=ids, dma_engine_mask=m, remote_sem=T.sem["arr%d" % s],
-                           srcs=[T.xd[:, :]], dsts=[T.xd[:, :] if to_helpers else _slot(T, s) for t in targets], alu_op=0)
-    g.remote_dma_fused([tr], local_sem=T.sem.sent)
+    hs = sorted(hh)
+    m = topo.mask(core, hh[hs[0]][0])
+    trs = []
+    for h, mm in zip(hs, _split(m, len(hs))):
+        ids = []
+        for t in hh[h]:
+            rid, pid = topo.addr(t, core)
+            ids.append(DstId(rid=rid, pnc=pid))
+        trs.append(RemoteDMATransfer(dst_ids=ids, dma_engine_mask=mm, remote_sem=T.sem["arr%d" % s], srcs=[T.xd[h]],
+                                     dsts=[T.xd[h] if to_helpers else _part(T, s, h) for t in hh[h]], alu_op=0))
+    g.remote_dma_fused(trs, local_sem=T.sem.sent)
     return _bits(m)
 
 
-def _pass_on(g, core, T, topo, cores, todo, origin):
+def _pass_on(g, core, T, topo, cores, todo, need):
     left = 0
     for s, d in todo:
-        g.wait_ge(T.sem["arr%d" % s], _bits(topo.mask(origin[(s, core)], core)))
+        g.wait_ge(T.sem["arr%d" % s], need[(s, core)])
         rid, pid = topo.addr(cores[d], core)
         m = topo.mask(core, cores[d])
         g.remote_dma(_slot(T, s), _slot(T, s), T.sem["arr%d" % s], T.sem.sent, pid, rid, m)
@@ -183,16 +230,16 @@ def _pass_on(g, core, T, topo, cores, todo, origin):
 
 def rank_program(g, core, T, topo):
     cores = list(T.cores)
-    send, helpers, fwd, origin = _plan(cores, topo)
+    send, helpers, fwd, need = _plan(cores, topo)
     rank = T.rank_of(core)
     if rank is None:
         if core in send:
-            s, targets = send[core]
-            g.wait_ge(T.sem["arr%d" % s], _bits(topo.mask(cores[s], core)))
-            left = _fan(g, core, T, topo, s, targets, False)
+            s, hh = send[core]
+            g.wait_ge(T.sem["arr%d" % s], need[(s, core)])
+            left = _fan(g, core, T, topo, s, hh, False)
             g.wait_ge(T.sem.sent, left)
         elif core in fwd:
-            left = _pass_on(g, core, T, topo, cores, fwd[core], origin)
+            left = _pass_on(g, core, T, topo, cores, fwd[core], need)
             g.wait_ge(T.sem.sent, left)
         return
 
@@ -200,7 +247,8 @@ def rank_program(g, core, T, topo):
     v, sc, pe, sy = g.vector, g.scalar, g.tensor, g.sync
     sem = T.sem
 
-    sy.dma_start(T.xd[:, :], T.x[:, :]).then_inc(sem.sxd, 16)
+    sy.dma_start(T.xd[0], T.x[:, 0:WH]).then_inc(sem.sxd, 16)
+    sc.dma_start(T.xd[1], T.x[:, WH:W]).then_inc(sem.sxd, 16)
     sy.dma_start(_slot(T, rank), T.x[:, :]).then_inc(sem.sx, 16)
     for t in range(3):
         sc.dma_start(T.lnsb[16 * t:16 * t + 16, :], T.ln[:, :]).then_inc(sem.sln, 16)
@@ -222,20 +270,22 @@ def rank_program(g, core, T, topo):
     V(v.memset(T.tri[:, :], 1.0))
     V(v.memset(T.kcol[:, :], float(W)))
     G(g.iota(T.pcol[:, 0:1], [[0, 1]], 0, 1))
-    G(g.iota(T.lhs[32:48, :], [[0, 8], [1, 16]], 0, 0, allow_small_or_imprecise_dtypes=True))
     g.wait_ge(sem.vs, 2)
     G(g.affine_select(T.tri[:, :], T.tri[:, :], [[0, 3], [1, 16]], A.is_ge, 0.0, 0, -1))
     g_tri = gc[0]
     G(g.affine_select(T.kcol[:, :], T.kcol[:, :], [[0, 1]], A.not_equal, 16896.0, -(N - 1), 1))
     G(g.affine_select(T.kcol[:, :], T.kcol[:, :], [[0, 1]], A.not_equal, 16896.0, -(32 + N - 1), 1))
+    g_kcol = gc[0]
 
-    g.wait_ge(sem.sxd, 16)
+    g.wait_ge(sem.sxd, 16 * H)
     far_h, near_h = helpers[rank]
     left = _fan(g, core, T, topo, rank, far_h, True)
     left += _fan(g, core, T, topo, rank, near_h, True)
     if core in send:
         left += _fan(g, core, T, topo, rank, send[core][1], False)
-    left += _pass_on(g, core, T, topo, cores, fwd.get(core, []), origin)
+    G(g.iota(T.lhs[32:48, :], [[0, 8], [1, 16]], 0, 0, allow_small_or_imprecise_dtypes=True))
+    g_lhs = gc[0]
+    left += _pass_on(g, core, T, topo, cores, fwd.get(core, []), need)
 
     V(v.memset(T.lhs[0:32, :], 1.0))
     V(v.memset(T.win[:, 0:Z], 0.0))
@@ -249,7 +299,7 @@ def rank_program(g, core, T, topo):
     pe.wait_ge(sem.vs, vc[0])
     pe.wait_ge(sem.gs, g_tri)
     pe.matmul(T.psa[0:48, 0:1], T.tri[0:16, 0:48], T.nf[0:16, 0:1], True, True).then_inc(sem.pe, 1)
-    v.wait_ge(sem.gs, gc[0])
+    v.wait_ge(sem.gs, g_kcol)
     V(v.tensor_scalar(T.scol[:, :], T.nf[:, :], T.kcol[:, 0:1], -1.0, A.add, A.mult))
     v.wait_ge(sem.pe, 1)
     V(v.tensor_copy(T.ei[:, :], T.psa[0:48, 0:1]))
@@ -258,6 +308,7 @@ def rank_program(g, core, T, topo):
     V(v.tensor_copy(T.abf[:, :], T.abi[:, :]))
     V(v.tensor_scalar(T.rhs[0:16, :], T.rhs[0:16, :], T.abf[0:16, 0:1], T.scol[0:16, 0:1], A.is_gt, A.mult))
     V(v.tensor_scalar(T.rhs[32:48, :], T.rhs[32:48, :], T.abf[32:48, 0:1], T.scol[32:48, 0:1], A.is_equal, A.mult))
+    v.wait_ge(sem.gs, g_lhs)
     V(v.tensor_scalar(T.lhs[32:48, :], T.lhs[32:48, :], T.abf[32:48, 1:2], None, A.is_ge))
     pe.wait_ge(sem.vs, vc[0])
     pe.matmul(T.psb[:, :], T.lhs[0:48, :], T.rhs[0:48, :], True, True).then_inc(sem.pe, 1)
@@ -265,9 +316,9 @@ def rank_program(g, core, T, topo):
     V(v.tensor_scalar(T.offs[:, :], T.psb[:, :], T.mcol[:, 0:1], 0.0, A.add, A.max))
 
     sc.wait_ge(sem.vs, vc[0])
+    pieces = [(k, 0, W, k % 2) for k in range(N - 1, 0, -1)] + [(0, 0, W // 2, 0), (0, W // 2, W, 1)]
     seen = {0: set(), 1: set()}
-    for k in range(N - 1, -1, -1):
-        e = k % 2
+    for k, a, b, e in pieces:
         q = v if e else sc
         for s in range(k, N):
             if s not in seen[e]:
@@ -275,16 +326,21 @@ def rank_program(g, core, T, topo):
                 if s == rank:
                     q.wait_ge(sem.sx, 16)
                 else:
-                    q.wait_ge(sem["arr%d" % s], _bits(topo.mask(origin[(s, core)], core)))
-        src = T.win[:, 0:Z + W * (N - k)].indirect(T.offs[:, QC * k:QC * (k + 1)])
-        dst = T.outb[:, W * k:W * (k + 1)]
+                    q.wait_ge(sem["arr%d" % s], need[(s, core)])
+        src = T.win[:, 0:Z + W * (N - k)].indirect(T.offs[:, QC * k + a // 16:QC * k + b // 16])
+        dst = T.outb[:, W * k + a:W * k + b]
+        dn = sem["done%d" % (k // 2)] if k > 1 else sem["last%d" % k]
         if e:
-            v.tensor_copy(dst, src).then_inc(sem["done%d" % (k // 2)], 1)
+            v.tensor_copy(dst, src).then_inc(dn, 1)
         else:
-            sc.activation(dst, src, ActivationFunctionType.Copy).then_inc(sem["done%d" % (k // 2)], 1)
+            sc.activation(dst, src, ActivationFunctionType.Copy).then_inc(dn, 1)
 
-    for i in range(N // 2 - 1, -1, -1):
+    for i in range(N // 2 - 1, 0, -1):
         sy.wait_ge(sem["done%d" % i], 2)
         sy.dma_start(T.y[:, 2 * W * i:2 * W * (i + 1)], T.outb[:, 2 * W * i:2 * W * (i + 1)]).then_inc(sem.st, 16)
-    sy.wait_ge(sem.st, 16 * (N // 2))
+    sy.wait_ge(sem.last1, 1)
+    sy.dma_start(T.y[:, W:2 * W], T.outb[:, W:2 * W]).then_inc(sem.st, 16)
+    sy.wait_ge(sem.last0, 2)
+    sy.dma_start(T.y[:, 0:W], T.outb[:, 0:W]).then_inc(sem.st, 16)
+    sy.wait_ge(sem.st, 16 * (N // 2 + 1))
     g.wait_ge(sem.sent, left)

from concourse.bass import DstId, RemoteDMATransfer
from concourse.mybir import AluOpType, ActivationFunctionType

N = 16
W = 512
Z = 8
QC = W // 16
LOW = 5
PAIR = 6
H = 2
WH = W // H

SCRATCH = {
    "win": ("sbuf", [128, Z + N * W], "bfloat16"),
    "xd": ("dram", [H, 128, WH], "bfloat16"),
    "outb": ("sbuf", [128, N * W], "bfloat16"),
    "offs": ("sbuf", [128, N * QC], "uint16"),
    "lnsb": ("sbuf", [48, 2], "int32"),
    "nf": ("sbuf", [48, 1], "float32"),
    "tri": ("sbuf", [16, 48], "float32"),
    "kcol": ("sbuf", [48, 1], "float32"),
    "scol": ("sbuf", [48, 1], "float32"),
    "ei": ("sbuf", [48, 1], "int32"),
    "abi": ("sbuf", [48, 2], "int32"),
    "abf": ("sbuf", [48, 2], "float32"),
    "ones": ("sbuf", [48, W], "float32"),
    "rhs": ("sbuf", [48, W], "float32"),
    "lhs": ("sbuf", [48, 128], "float32"),
    "pcol": ("sbuf", [128, 1], "int32"),
    "pmi": ("sbuf", [128, 1], "int32"),
    "mcol": ("sbuf", [128, 1], "float32"),
    "psa": ("psum", [128, 512], "float32"),
    "psb": ("psum", [128, 512], "float32"),
}
SEMAPHORES = ["sx", "sxd", "sln", "st", "vs", "gs", "pe", "sent", "last0", "last1"] + \
             ["arr%d" % s for s in range(N)] + ["done%d" % i for i in range(1, N // 2)]

_PLAN = {}


def _bits(m):
    return bin(m).count("1")


def _plan(cores, topo):
    if "p" in _PLAN:
        return _PLAN["p"]
    n = len(cores)
    world = range(topo.CORES_PER_HOST * (1 + max(topo.host(c) for c in cores)))

    def ck(c):
        return (topo.host(c), topo.chip(c))

    chipc = {}
    for c in world:
        chipc.setdefault(ck(c), []).append(c)
    mate = {}
    for a in chipc:
        for b in chipc:
            if topo.mates(chipc[a][0], chipc[b][0]):
                mate[a] = b
    busy = {}
    for r, c in enumerate(cores):
        busy[ck(c)] = r
    load = {}

    def route(a, b):
        d = topo.die(a)
        if ck(a) == ck(b):
            return []
        if topo.same_plane(a, b):
            return [("out", ck(a), d), ("in", ck(b), d)]
        r = [("mate", ck(a), d)]
        if mate[ck(a)] != ck(b):
            r += [("out", mate[ck(a)], d), ("in", ck(b), d)]
        return r

    def charge(a, b, u):
        for l in route(a, b):
            load[l] = load.get(l, 0) + u

    fwd = {}
    jobs = []
    skip = set()
    low = list(range(n))[:LOW]
    pairs = []
    for d, cd in enumerate(cores):
        m = mate[ck(cd)]
        if m in busy:
            if d < busy[m]:
                pairs.append((d, busy[m]))
            continue
        door = [c for c in chipc[m] if topo.may_write(c, cd)]
        for s in low:
            if s == d:
                continue
            f = min(door, key=lambda c: (len(fwd.get(c, [])), load.get(("mate", m, topo.die(c)), 0), c))
            fwd.setdefault(f, []).append((s, d))
            skip.add((s, d))
            charge(f, cd, H)
            jobs.append((s, f))

    def cross(r):
        tg = [t for (a, t) in jobs if a == r] + [cores[q] for q in range(n) if q != r and (r, q) not in skip]
        return sum(1 for t in tg if not topo.same_plane(cores[r], t) and not topo.mates(cores[r], t))

    for d, e in pairs:
        f, o = (d, e) if cross(d) > cross(e) else (e, d)
        ls = [s for s in range(n) if s not in (d, e)][:PAIR]
        for i, s in enumerate(ls):
            a, b = (f, o) if i % 3 == 1 else (o, f)
            fwd.setdefault(cores[a], []).append((s, b))
            skip.add((s, b))
            charge(cores[a], cores[b], H)
    for dl in range(1, n):
        for s in range(n):
            d = (s + dl) % n
            if (s, d) not in skip:
                jobs.append((s, cores[d]))

    pools = {}
    taken = set()
    half = {}
    for s, cs in enumerate(cores):
        tg = [t for (a, t) in jobs if a == s]
        far = [t for t in tg if not topo.same_plane(cs, t) and not topo.mates(cs, t)]
        relay = []
        if mate[ck(cs)] in busy and 2 * len(far) > len(tg):
            for k in sorted(chipc):
                if (k[0] == topo.host(cs) and k not in busy and mate[k] not in busy and k not in taken
                        and all(topo.same_plane(chipc[k][0], t) for t in far)):
                    taken.add(k)
                    for die in sorted(set(topo.die(c) for c in chipc[k])):
                        relay += [c for c in chipc[k] if topo.die(c) == die][:2]
                    break
        for i, c in enumerate(relay):
            charge(cs, c, 1)
            half[c] = i % H
        probe = chipc[mate[ck(cs)]][0]
        own = sorted(chipc[ck(cs)], key=lambda c: (not topo.may_write(c, probe), topo.die(c), c))
        for i, c in enumerate(own):
            half[c] = i % H
        pools[s] = (own, relay, set(far) if relay else set())
    work = {c: H for c in cores}
    send = {}
    jobs.sort(key=lambda p: topo.same_plane(cores[p[0]], p[1]))
    for s, t in jobs:
        own, relay, far = pools[s]
        for h in range(H):
            if topo.mates(cores[s], t):
                cand = [cores[s]]
            elif t in far:
                cand = [c for c in relay if half[c] == h]
            else:
                cand = [c for c in own if topo.may_write(c, t) and (c == cores[s] or half[c] == h)]
            best = min(cand, key=lambda c: (max(load.get(l, 0) for l in route(c, t)), work.get(c, 0), c))
            charge(best, t, 1)
            work[best] = work.get(best, 0) + 1
            send.setdefault(best, (s, {}))[1].setdefault(h, []).append(t)
    helpers = {}
    for s, cs in enumerate(cores):
        grp = ({}, {})
        for c in sorted(send):
            if send[c][0] == s and c != cs:
                grp[ck(c) == ck(cs)].setdefault(half[c], []).append(c)
        helpers[s] = grp
    for f in fwd:
        fwd[f].sort(key=lambda p: -p[0])
    need = {}
    for c in send:
        s, hh = send[c]
        for h in hh:
            for t in hh[h]:
                need[(s, t)] = need.get((s, t), 0) + _bits(topo.mask(c, t)) // len(hh)
    for s, cs in enumerate(cores):
        for grp in helpers[s]:
            for h in grp:
                for c in grp[h]:
                    need[(s, c)] = _bits(topo.mask(cs, c)) // len(grp)
    for f in fwd:
        for s, d in fwd[f]:
            need[(s, cores[d])] = need.get((s, cores[d]), 0) + _bits(topo.mask(f, cores[d]))
    _PLAN["p"] = (send, helpers, fwd, need)
    return _PLAN["p"]


def _slot(T, s):
    a = Z + W * (N - 1 - s)
    return T.win[:, a:a + W]


def _part(T, s, h):
    a = Z + W * (N - 1 - s) + WH * h
    return T.win[:, a:a + WH]


def _split(m, parts):
    bl = [1 << i for i in range(m.bit_length()) if (m >> i) & 1]
    k = len(bl) // parts
    return [sum(bl[i * k:(i + 1) * k]) for i in range(parts)]


def _fan(g, core, T, topo, s, hh, to_helpers):
    if not hh:
        return 0
    hs = sorted(hh)
    m = topo.mask(core, hh[hs[0]][0])
    trs = []
    for h, mm in zip(hs, _split(m, len(hs))):
        ids = []
        for t in hh[h]:
            rid, pid = topo.addr(t, core)
            ids.append(DstId(rid=rid, pnc=pid))
        trs.append(RemoteDMATransfer(dst_ids=ids, dma_engine_mask=mm, remote_sem=T.sem["arr%d" % s], srcs=[T.xd[h]],
                                     dsts=[T.xd[h] if to_helpers else _part(T, s, h) for t in hh[h]], alu_op=0))
    g.remote_dma_fused(trs, local_sem=T.sem.sent)
    return _bits(m)


def _pass_on(g, core, T, topo, cores, todo, need):
    left = 0
    for s, d in todo:
        g.wait_ge(T.sem["arr%d" % s], need[(s, core)])
        rid, pid = topo.addr(cores[d], core)
        m = topo.mask(core, cores[d])
        g.remote_dma(_slot(T, s), _slot(T, s), T.sem["arr%d" % s], T.sem.sent, pid, rid, m)
        left += _bits(m)
    return left


def rank_program(g, core, T, topo):
    cores = list(T.cores)
    send, helpers, fwd, need = _plan(cores, topo)
    rank = T.rank_of(core)
    if rank is None:
        if core in send:
            s, hh = send[core]
            g.wait_ge(T.sem["arr%d" % s], need[(s, core)])
            left = _fan(g, core, T, topo, s, hh, False)
            g.wait_ge(T.sem.sent, left)
        elif core in fwd:
            left = _pass_on(g, core, T, topo, cores, fwd[core], need)
            g.wait_ge(T.sem.sent, left)
        return

    A = AluOpType
    v, sc, pe, sy = g.vector, g.scalar, g.tensor, g.sync
    sem = T.sem

    sy.dma_start(T.xd[0], T.x[:, 0:WH]).then_inc(sem.sxd, 16)
    sc.dma_start(T.xd[1], T.x[:, WH:W]).then_inc(sem.sxd, 16)
    sy.dma_start(_slot(T, rank), T.x[:, :]).then_inc(sem.sx, 16)
    for t in range(3):
        sc.dma_start(T.lnsb[16 * t:16 * t + 16, :], T.ln[:, :]).then_inc(sem.sln, 16)

    vc = [0]

    def V(ins):
        ins.then_inc(sem.vs, 1)
        vc[0] += 1
        v.wait_ge(sem.vs, vc[0])

    gc = [0]

    def G(ins):
        ins.then_inc(sem.gs, 1)
        gc[0] += 1
        g.wait_ge(sem.gs, gc[0])

    V(v.memset(T.tri[:, :], 1.0))
    V(v.memset(T.kcol[:, :], float(W)))
    G(g.iota(T.pcol[:, 0:1], [[0, 1]], 0, 1))
    g.wait_ge(sem.vs, 2)
    G(g.affine_select(T.tri[:, :], T.tri[:, :], [[0, 3], [1, 16]], A.is_ge, 0.0, 0, -1))
    g_tri = gc[0]
    G(g.affine_select(T.kcol[:, :], T.kcol[:, :], [[0, 1]], A.not_equal, 16896.0, -(N - 1), 1))
    G(g.affine_select(T.kcol[:, :], T.kcol[:, :], [[0, 1]], A.not_equal, 16896.0, -(32 + N - 1), 1))
    g_kcol = gc[0]

    g.wait_ge(sem.sxd, 16 * H)
    far_h, near_h = helpers[rank]
    left = _fan(g, core, T, topo, rank, far_h, True)
    left += _fan(g, core, T, topo, rank, near_h, True)
    if core in send:
        left += _fan(g, core, T, topo, rank, send[core][1], False)
    G(g.iota(T.lhs[32:48, :], [[0, 8], [1, 16]], 0, 0, allow_small_or_imprecise_dtypes=True))
    g_lhs = gc[0]
    left += _pass_on(g, core, T, topo, cores, fwd.get(core, []), need)

    V(v.memset(T.lhs[0:32, :], 1.0))
    V(v.memset(T.win[:, 0:Z], 0.0))
    V(v.memset(T.ones[:, :], 1.0))
    V(v.tensor_tensor_scan(T.rhs[:, :], T.ones[:, :], T.ones[:, :], -1.0, A.mult, A.add))
    v.wait_ge(sem.gs, 1)
    V(v.tensor_scalar(T.pmi[:, :], T.pcol[:, :], 15, None, A.bitwise_and))
    V(v.tensor_scalar(T.mcol[:, :], T.pmi[:, :], float(Z + W * (N - 1)), None, A.add))
    v.wait_ge(sem.sln, 48)
    V(v.tensor_copy(T.nf[:, :], T.lnsb[:, 0:1]))
    pe.wait_ge(sem.vs, vc[0])
    pe.wait_ge(sem.gs, g_tri)
    pe.matmul(T.psa[0:48, 0:1], T.tri[0:16, 0:48], T.nf[0:16, 0:1], True, True).then_inc(sem.pe, 1)
    v.wait_ge(sem.gs, g_kcol)
    V(v.tensor_scalar(T.scol[:, :], T.nf[:, :], T.kcol[:, 0:1], -1.0, A.add, A.mult))
    v.wait_ge(sem.pe, 1)
    V(v.tensor_copy(T.ei[:, :], T.psa[0:48, 0:1]))
    V(v.tensor_scalar(T.abi[:, 0:1], T.ei[:, :], 4, None, A.arith_shift_right))
    V(v.tensor_scalar(T.abi[:, 1:2], T.ei[:, :], 15, None, A.bitwise_and))
    V(v.tensor_copy(T.abf[:, :], T.abi[:, :]))
    V(v.tensor_scalar(T.rhs[0:16, :], T.rhs[0:16, :], T.abf[0:16, 0:1], T.scol[0:16, 0:1], A.is_gt, A.mult))
    V(v.tensor_scalar(T.rhs[32:48, :], T.rhs[32:48, :], T.abf[32:48, 0:1], T.scol[32:48, 0:1], A.is_equal, A.mult))
    v.wait_ge(sem.gs, g_lhs)
    V(v.tensor_scalar(T.lhs[32:48, :], T.lhs[32:48, :], T.abf[32:48, 1:2], None, A.is_ge))
    pe.wait_ge(sem.vs, vc[0])
    pe.matmul(T.psb[:, :], T.lhs[0:48, :], T.rhs[0:48, :], True, True).then_inc(sem.pe, 1)
    v.wait_ge(sem.pe, 2)
    V(v.tensor_scalar(T.offs[:, :], T.psb[:, :], T.mcol[:, 0:1], 0.0, A.add, A.max))

    sc.wait_ge(sem.vs, vc[0])
    pieces = [(k, 0, W, k % 2) for k in range(N - 1, 0, -1)] + [(0, 0, W // 2, 0), (0, W // 2, W, 1)]
    seen = {0: set(), 1: set()}
    for k, a, b, e in pieces:
        q = v if e else sc
        for s in range(k, N):
            if s not in seen[e]:
                seen[e].add(s)
                if s == rank:
                    q.wait_ge(sem.sx, 16)
                else:
                    q.wait_ge(sem["arr%d" % s], need[(s, core)])
        src = T.win[:, 0:Z + W * (N - k)].indirect(T.offs[:, QC * k + a // 16:QC * k + b // 16])
        dst = T.outb[:, W * k + a:W * k + b]
        dn = sem["done%d" % (k // 2)] if k > 1 else sem["last%d" % k]
        if e:
            v.tensor_copy(dst, src).then_inc(dn, 1)
        else:
            sc.activation(dst, src, ActivationFunctionType.Copy).then_inc(dn, 1)

    for i in range(N // 2 - 1, 0, -1):
        sy.wait_ge(sem["done%d" % i], 2)
        sy.dma_start(T.y[:, 2 * W * i:2 * W * (i + 1)], T.outb[:, 2 * W * i:2 * W * (i + 1)]).then_inc(sem.st, 16)
    sy.wait_ge(sem.last1, 1)
    sy.dma_start(T.y[:, W:2 * W], T.outb[:, W:2 * W]).then_inc(sem.st, 16)
    sy.wait_ge(sem.last0, 2)
    sy.dma_start(T.y[:, 0:W], T.outb[:, 0:W]).then_inc(sem.st, 16)
    sy.wait_ge(sem.st, 16 * (N // 2 + 1))
    g.wait_ge(sem.sent, left)
